import numpy as np
import ml_dtypes


def mxq(x, axis, fmt="e4m3"):
    dtype, down = {"e4m3": (ml_dtypes.float8_e4m3fn, 7), "e5m2": (ml_dtypes.float8_e5m2, 14)}[fmt]
    v = np.moveaxis(np.asarray(x, np.float32).astype(ml_dtypes.bfloat16).astype(np.float64), axis, -1)
    blocks = v.reshape(v.shape[:-1] + (-1, 32))
    amax = np.abs(blocks).max(-1, keepdims=True)
    byte = np.maximum(np.where(amax > 0, np.frexp(amax)[1] - 1 + 127, 0) - down, 1)
    scale = np.exp2(byte - 127.0)
    codes = (blocks / scale).astype(np.float32).astype(dtype).astype(np.float64)
    return np.moveaxis((codes * scale).reshape(v.shape), -1, axis)


WIDE = False


def mx_kscale(k):
    if not WIDE:
        return np.ones(k)
    levels = np.array([10, -10, 5, -5, 0])
    if k % 512:
        return np.exp2(np.random.permutation(np.resize(levels, k // 32))).repeat(32)
    a = np.empty((k // 512, 16))
    for p in range(k // 512):
        a[p, :8] = np.random.permutation(np.resize(levels, 8))
        for g in range(8):
            far = levels[np.abs(levels - a[p, g]) >= 10]
            a[p, g + 8] = far[np.random.randint(len(far))]
    return np.exp2(a.ravel()).repeat(32)


def f64(x):
    return np.asarray(x).astype(np.float64)


def striped(idx):
    return np.tile(idx.reshape(-1, 16).T, (8, 1)).astype(np.uint16)


def unstriped(offs):
    return offs[:16].T.reshape(-1).astype(np.int64)


def striped8(idx):
    return np.concatenate([x.reshape(-1, 16).T for x in idx]).astype(np.uint16)


def runs(offs, k):
    lists = np.stack([offs[16 * r : 16 * r + 16].T.reshape(-1) for r in range(8)]).astype(np.int64)
    return lists[np.arange(k) % 512 // 64]


def pack_weight(w):
    k, n = w.shape
    w = f64(np.asarray(w, np.float32).astype(ml_dtypes.bfloat16)).reshape(k // 32, 32, n)
    amax = np.abs(w).max(1)
    byte = np.clip(np.where(amax > 0, np.frexp(amax)[1] - 1 + 127 - 7, 1), 1, 254)
    scaled = (w * np.exp2(127.0 - byte)[:, None, :]).reshape(k, n).astype(np.float32)
    words = np.ascontiguousarray(scaled.reshape(k // 512, 128, 4, n).transpose(0, 1, 3, 2)).astype(ml_dtypes.float8_e4m3fn).view(np.uint8)
    return words, np.ascontiguousarray(byte.astype(np.uint8).reshape(k // 512, 16, n))


def unpack_weight(words, scales):
    g, p, n, _ = words.shape
    vals = np.ascontiguousarray(words).view(ml_dtypes.float8_e4m3fn).astype(np.float64) * np.repeat(np.exp2(scales.astype(np.float64) - 127.0), 8, axis=1)[..., None]
    return vals.transpose(0, 1, 3, 2).reshape(g * 512, n)


def sigmoid(v):
    return 1.0 / (1.0 + np.exp(-np.maximum(v, -700.0)))


K, T, S, V, H, W = 512, 2048, 512, 512, 512, 256


def setup_inputs():
    n = np.random.standard_normal
    s = mx_kscale(K)[:, None]
    u = mx_kscale(S)
    packed_xT = pack_weight(n((K, T)) * s)
    perm = np.stack([np.random.permutation(V) for _ in range(8)])
    return {
        "x_words": packed_xT[0],
        "x_scales": packed_xT[1],
        "w1": (n((K, H)) / np.sqrt(K) / s).astype(np.float32),
        "w2": (n((K, H)) / np.sqrt(K) / s).astype(np.float32),
        "ga": (np.random.uniform(0.5, 1.5, (H, 1)) * u[:, None]).astype(np.float32),
        "gb": (np.random.uniform(0.5, 1.5, (H, 1)) / u[:, None]).astype(np.float32),
        "offs": striped(np.random.permutation(T)[:S]),
        "two": striped(np.random.permutation(T)[:V]),
        "n1": striped8(np.stack([np.random.permutation(S) for _ in range(8)])),
        "n2": striped8(np.stack([np.random.permutation(V) for _ in range(8)])),
        "n3": striped8(np.stack([np.random.permutation(V) for _ in range(8)])),
        "n4": striped8(perm[:, :W]),
        "n5": striped8(perm[:, W:]),
    }


def reference(x_words, x_scales, w1, w2, ga, gb, offs, two, n1, n2, n3, n4, n5):
    xq = unpack_weight(x_words, x_scales)[:, unstriped(offs)]
    a = mxq(f64(w1), 0, "e4m3").T @ xq
    st = a * (sigmoid(a[np.arange(H)[:, None], runs(n1, H)]))
    z = f64(ga) * (np.maximum(st, st[np.arange(H)[:, None], runs(n1, H)]))
    x_two = unpack_weight(x_words, x_scales)[:, unstriped(two)]
    b = mxq(f64(w2), 0, "e4m3").T @ x_two
    st2 = b + 0.5 * (b[np.arange(H)[:, None], runs(n2, H)])
    z2 = f64(gb) * (st2 - (st2[np.arange(H)[:, None], runs(n3, H)]))
    s = 0.0625 * ((mxq(z, 0, "e4m3").T @ mxq(z2, 0, "e4m3")))
    pa = s[np.arange(S)[:, None], runs(n4, S)]
    pb = s[np.arange(S)[:, None], runs(n5, S)]
    rb = np.minimum(pa, pb)
    ra = np.maximum(pa, pb)
    ds = np.zeros((S, V))
    ds[np.arange(S)[:, None], runs(n4, S)] = ra
    out = ds.copy()
    out[np.arange(S)[:, None], runs(n5, S)] = rb
    return out

@@ -1,0 +1,265 @@
+from contextlib import ExitStack
+
+import concourse.mybir as mybir
+
+F32 = mybir.dt.float32
+BF16 = mybir.dt.bfloat16
+I32 = mybir.dt.int32
+U32 = mybir.dt.uint32
+U16 = mybir.dt.uint16
+U8 = mybir.dt.uint8
+FP8X4 = mybir.dt.float8_e4m3fn_x4
+ALU = mybir.AluOpType
+ACT = mybir.ActivationFunctionType
+
+P = 128
+PACK = 4
+T = 2048
+N = 512
+HALF = 256
+FLOPS = 3 * 2 * 512 * 512 * 512
+
+
+def tile_picked_kqtwicphoporder_none_p_kernel(
+    tc, x_words, x_scales, w1, w2, ga, gb, offs, two, n1, n2, n3, n4, n5, out
+):
+    nc = tc.nc
+    with ExitStack() as ctx:
+        held = ctx.enter_context(tc.tile_pool(name="held", bufs=1))
+        psum = ctx.enter_context(tc.psum_pool(name="psum", bufs=8))
+
+        def load_list(name, src):
+            tile = held.tile(list(src.shape), U16, name=name)
+            nc.sync.dma_start(tile[:], src)
+            return tile
+
+        def half_of(lst, h):
+            return lst[:, 16 * h : 16 * (h + 1)]
+
+        xs_all = held.tile([P, T], U8, name="xs_all")
+        nc.vector.memset(xs_all[:].bitcast(U32), 0)
+        warm = held.tile([P, 1], F32, name="warm")
+        nc.gpsimd.memset(warm[:], 0.0)
+        warm_out = held.tile([P, 1], F32, name="warm_out")
+        nc.scalar.activation(warm_out[:], warm[:], ACT.Sigmoid)
+
+        def load_weight(w):
+            rows = w.rearrange("(p j) c -> p j c", j=PACK)
+            halves = []
+            for h in range(2):
+                raw = held.tile([P, PACK, HALF], F32, name="w_raw%d" % h)
+                nc.sync.dma_start(raw[:], rows[:, :, HALF * h : HALF * (h + 1)])
+                halves.append(raw)
+            return halves
+
+        xs_rows = held.tile([P, T], U8, name="xs_rows")
+        for q in range(4):
+            nc.sync.dma_start(xs_rows[32 * q : 32 * q + 4, :].bitcast(I32), x_scales[0, 4 * q : 4 * q + 4, :].bitcast(I32))
+        two_l = load_list("two_l", two)
+        w2_raw = load_weight(w2)
+        for q in range(4):
+            nc.vector.tensor_copy(xs_all[32 * q : 32 * q + 4, :].bitcast(I32), xs_rows[32 * q : 32 * q + 4, :].bitcast(I32))
+        xw_all = held.tile([P, T], I32, name="xw_all")
+        nc.sync.dma_start(xw_all[:], x_words[0].rearrange("p n r -> p (n r)").bitcast(I32))
+        gb_t = held.tile([P, PACK], F32, name="gb_t")
+        ga_t = held.tile([P, PACK], F32, name="ga_t")
+        nc.sync.dma_start(gb_t[:], gb.rearrange("(p t) o -> p (t o)", t=PACK))
+        nc.sync.dma_start(ga_t[:], ga.rearrange("(p t) o -> p (t o)", t=PACK))
+        offs_l = load_list("offs_l", offs)
+        n2_l = load_list("n2_l", n2)
+        n3_l = load_list("n3_l", n3)
+        n1_l = load_list("n1_l", n1)
+        n4_l = load_list("n4_l", n4)
+        n5_l = load_list("n5_l", n5)
+
+        step = held.tile([P, PACK], F32, name="step")
+        ga_abs = held.tile([P, PACK], F32, name="ga_abs")
+        gb_full = held.tile([P, PACK], F32, name="gb_full")
+        gb_half = held.tile([P, PACK], F32, name="gb_half")
+
+        def pick_scales(name, lst):
+            scales = held.tile([P, N], U8, name=name, align_bytes=64)
+            nc.vector.tensor_copy(scales[:], xs_all[:].indirect(lst[:]))
+            return scales
+
+        def pick_words(name, lst):
+            words = held.tile([P, N], U32, name=name, align_bytes=64)
+            for h in range(2):
+                nc.vector.tensor_copy(words[:, HALF * h : HALF * (h + 1)], xw_all[:].bitcast(U32).indirect(half_of(lst, h)))
+            return words
+
+        def deal(copy, dst, src, m0, m1, src0):
+            copy(
+                dst[:, :, m0:m1, :].rearrange("p t m j -> p m j t"),
+                src.rearrange("p j (m t) -> p m j t", t=PACK)[:, m0 - src0 : m1 - src0, :, :],
+            )
+
+        def mx_tiles(name):
+            grouped = held.tile([P, PACK, P, PACK], BF16, name=name + "_g", align_bytes=64)
+            words = held.tile([P, N], U32, name=name + "_w", align_bytes=64)
+            scales = held.tile([P, N], U8, name=name + "_s", align_bytes=64)
+            return grouped, words, scales
+
+        def quantise(grouped, words, scales, t0, t1):
+            nc.vector.quantize_mx(
+                out=words[:, P * t0 : P * t1].bitcast(FP8X4),
+                scales=scales[:, P * t0 : P * t1],
+                in_=grouped[:, t0:t1].rearrange("p t m j -> p (t m j)"),
+            )
+
+        def product(tag, lw, ls, rw, rs, t, cols=slice(0, N)):
+            bank = psum.tile([P, cols.stop - cols.start], F32, name=tag)
+            nc.tensor.matmul_mx(
+                out=bank[:],
+                lhsT=lw[:, P * t : P * (t + 1)].bitcast(FP8X4),
+                lhsT_scale=ls[:, P * t : P * (t + 1)],
+                rhs=rw[:, cols].bitcast(FP8X4),
+                rhs_scale=rs[:, cols],
+                start=True,
+                stop=True,
+            )
+            return bank
+
+        xt_s = pick_scales("xt_s", two_l)
+        w2_g, w2_w, w2_s = mx_tiles("w2")
+        deal(nc.scalar.copy, w2_g, w2_raw[0][:], 0, 64, 0)
+        deal(nc.scalar.copy, w2_g, w2_raw[1][:], 64, 96, 64)
+        deal(nc.vector.tensor_copy, w2_g, w2_raw[1][:], 96, 128, 64)
+        quantise(w2_g, w2_w, w2_s, 0, 4)
+        w1_raw = load_weight(w1)
+        xt_w = pick_words("xt_w", two_l)
+        nc.vector.tensor_scalar(step[:], ga_t[:], 0.0, -0.5, ALU.is_ge, ALU.add)
+        nc.vector.scalar_tensor_tensor(ga_abs[:], ga_t[:], -1.0, ga_t[:], ALU.mult, ALU.max)
+        nc.vector.tensor_tensor(gb_half[:], step[:], gb_t[:], ALU.mult)
+        nc.vector.tensor_scalar(gb_full[:], gb_half[:], 2.0, None, ALU.mult)
+        xo_s = pick_scales("xo_s", offs_l)
+        xo_w = pick_words("xo_w", offs_l)
+
+        st2 = []
+        st2_copy = []
+        for t in range(PACK):
+            b_half = held.tile([P, N], F32, name="b_half%d" % t)
+            b_full = held.tile([P, N], F32, name="b_full%d" % t)
+            width = HALF if t == 0 else N
+            for c in range(0, N, width):
+                cols = slice(c, c + width)
+                bank = product("bank", w2_w, w2_s, xt_w, xt_s, t, cols)
+                nc.scalar.activation(b_half[:, cols], bank[:], ACT.Copy, scale=gb_half[:, t : t + 1])
+                nc.scalar.activation(b_full[:, cols], bank[:], ACT.Copy, scale=gb_full[:, t : t + 1])
+            s2 = held.tile([P, N], F32, name="st2_%d" % t)
+            s2c = held.tile([P, N], F32, name="st2c_%d" % t)
+            for h in range(2):
+                cols = slice(HALF * h, HALF * (h + 1))
+                nc.vector.tensor_tensor(s2[:, cols], b_half[:].indirect(half_of(n2_l, h)), b_full[:, cols], ALU.add)
+            nc.sync.dma_start(s2c[:], s2[:])
+            st2.append(s2)
+            st2_copy.append(s2c)
+
+        w1_g, w1_w, w1_s = mx_tiles("w1")
+        deal(nc.scalar.copy, w1_g, w1_raw[0][:], 0, 64, 0)
+        deal(nc.scalar.copy, w1_g, w1_raw[1][:], 64, 128, 64)
+
+        z2 = []
+        for h in range(2):
+            cols = slice(HALF * h, HALF * (h + 1))
+            if h == 1:
+                quantise(w1_g, w1_w, w1_s, 0, 1)
+                quantise(w1_g, w1_w, w1_s, 1, 2)
+                quantise(w1_g, w1_w, w1_s, 2, 4)
+            z2_h = held.tile([P, PACK, HALF], F32, name="z2_%d" % h, tag=("z2_0", "w1_g")[h], align_bytes=64)
+            for t in range(PACK):
+                nc.vector.tensor_tensor(z2_h[:, t, :], st2[t][:].indirect(half_of(n3_l, h)), st2_copy[t][:, cols], ALU.subtract)
+            z2.append(z2_h)
+
+        z2_w = held.tile([P, N], U32, name="z2_w", align_bytes=64)
+        z2_s = held.tile([P, N], U8, name="z2_s", align_bytes=64)
+
+        def weave_z2(h, tag):
+            grouped = held.tile([P, HALF, PACK], BF16, name="z2_g%d" % h, tag=tag, align_bytes=64)
+            nc.scalar.copy(
+                grouped[:].rearrange("p (c i) t -> p c t i", i=4),
+                z2[h][:].rearrange("p t (c i) -> p c t i", i=4),
+            )
+            return grouped
+
+        def quantise_z2(h, grouped):
+            cols = slice(HALF * h, HALF * (h + 1))
+            nc.vector.quantize_mx(out=z2_w[:, cols].bitcast(FP8X4), scales=z2_s[:, cols], in_=grouped[:].rearrange("p c t -> p (c t)"))
+
+        z2_g0 = weave_z2(0, "z2_g0")
+
+        z = held.tile([P, PACK, N], BF16, name="z")
+        st = []
+        looked = held.tile([P, PACK, N], F32, name="looked")
+
+        def larger(t, h):
+            cols = slice(HALF * h, HALF * (h + 1))
+            nc.vector.tensor_copy(looked[:, t, cols], st[t][:].indirect(half_of(n1_l, h)))
+
+        def larger2(t, h):
+            cols = slice(HALF * h, HALF * (h + 1))
+            nc.vector.tensor_tensor(z[:, t, cols], st[t][:, cols], looked[:, t, cols], ALU.max)
+
+        for t in range(PACK):
+            bank = product("bank", w1_w, w1_s, xo_w, xo_s, t)
+            a_sb = held.tile([P, N], F32, name="a%d" % t, align_bytes=64)
+            nc.scalar.copy(a_sb[:], bank[:])
+            gate = held.tile([P, N], F32, name="gate%d" % t)
+            for h in range(2):
+                cols = slice(HALF * h, HALF * (h + 1))
+                nc.scalar.activation(gate[:, cols], a_sb[:].indirect(half_of(n1_l, h)), ACT.Sigmoid)
+            s1 = held.tile([P, N], F32, name="st%d" % t)
+            nc.vector.scalar_tensor_tensor(s1[:], bank[:], ga_abs[:, t : t + 1], gate[:], ALU.mult, ALU.mult)
+            st.append(s1)
+            if t in (1, 2):
+                larger2(t - 1, 1)
+            larger(t, 0)
+            if t == 3:
+                larger2(2, 0)
+            if t < 2:
+                larger(t, 1)
+                larger2(t, 0)
+            if t == 0:
+                quantise_z2(0, z2_g0)
+
+        z2_g1 = weave_z2(1, "a3")
+        z_g, z_w, z_s = mx_tiles("z")
+        larger(2, 1)
+        larger2(3, 0)
+        deal(nc.scalar.copy, z_g, z[:], 0, 64, 0)
+        larger(3, 1)
+        larger2(2, 1)
+        quantise_z2(1, z2_g1)
+        larger2(3, 1)
+        deal(nc.scalar.copy, z_g, z[:], 64, 88, 0)
+        deal(nc.vector.tensor_copy, z_g, z[:], 88, 128, 0)
+        for t0, t1 in ((0, 1), (1, 2), (2, 4)):
+            quantise(z_g, z_w, z_s, t0, t1)
+
+        out_rows = out.rearrange("(m t) v -> t m v", t=PACK)
+        pending = []
+
+        def put_back(t, pa, up, down):
+            res = held.tile([P, N], F32, name="res%d" % t)
+            nc.vector.tensor_tensor(res[:].indirect(n4_l[:]), pa[:], up[:], ALU.add)
+            nc.vector.tensor_tensor(res[:].indirect(n5_l[:]), pa[:], down[:], ALU.add)
+            nc.sync.dma_start(out_rows[t], res[:])
+
+        for t in range(PACK):
+            bank = product("bank", z_w, z_s, z2_w, z2_s, t)
+            s_sb = held.tile([P, N], F32, name="s%d" % t)
+            nc.scalar.activation(s_sb[:], bank[:], ACT.Copy, scale=-0.0625)
+            pa = held.tile([P, HALF], F32, name="pa%d" % t)
+            gap = held.tile([P, HALF], F32, name="gap%d" % t)
+            up = held.tile([P, HALF], F32, name="up%d" % t)
+            lack = held.tile([P, HALF], F32, name="lack%d" % t)
+            down = held.tile([P, HALF], F32, name="down%d" % t)
+            nc.vector.tensor_copy(pa[:], s_sb[:].indirect(n4_l[:]))
+            nc.vector.tensor_tensor(gap[:], s_sb[:].indirect(n5_l[:]), pa[:], ALU.subtract)
+            nc.scalar.activation(up[:], gap[:], ACT.Relu)
+            nc.scalar.activation(lack[:], gap[:], ACT.Relu, scale=-1.0)
+            nc.scalar.activation(down[:], lack[:], ACT.Copy, scale=-1.0)
+            if pending:
+                put_back(*pending.pop())
+            pending.append((t, pa, up, down))
+        put_back(*pending.pop())

@@ -43,29 +43,26 @@ def tile_picked_kqtwicphoporder_none_p_kernel(
         warm_out = held.tile([P, 1], F32, name="warm_out")
         nc.scalar.activation(warm_out[:], warm[:], ACT.Sigmoid)
 
-        def load_weight(w):
-            rows = w.rearrange("(p j) c -> p j c", j=PACK)
-            halves = []
-            for h in range(2):
-                raw = held.tile([P, PACK, HALF], F32, name="w_raw%d" % h)
-                nc.sync.dma_start(raw[:], rows[:, :, HALF * h : HALF * (h + 1)])
-                halves.append(raw)
-            return halves
+        def load_weight_half(w, h):
+            raw = held.tile([P, PACK, HALF], F32, name="w_raw%d" % h)
+            nc.sync.dma_start(raw[:], w.rearrange("(p j) c -> p j c", j=PACK)[:, :, HALF * h : HALF * (h + 1)])
+            return raw
 
         xs_rows = held.tile([P, T], U8, name="xs_rows")
         for q in range(4):
             nc.sync.dma_start(xs_rows[32 * q : 32 * q + 4, :].bitcast(I32), x_scales[0, 4 * q : 4 * q + 4, :].bitcast(I32))
         two_l = load_list("two_l", two)
-        w2_raw = load_weight(w2)
-        for q in range(4):
-            nc.vector.tensor_copy(xs_all[32 * q : 32 * q + 4, :].bitcast(I32), xs_rows[32 * q : 32 * q + 4, :].bitcast(I32))
-        xw_all = held.tile([P, T], I32, name="xw_all")
-        nc.sync.dma_start(xw_all[:], x_words[0].rearrange("p n r -> p (n r)").bitcast(I32))
         gb_t = held.tile([P, PACK], F32, name="gb_t")
         ga_t = held.tile([P, PACK], F32, name="ga_t")
         nc.sync.dma_start(gb_t[:], gb.rearrange("(p t) o -> p (t o)", t=PACK))
         nc.sync.dma_start(ga_t[:], ga.rearrange("(p t) o -> p (t o)", t=PACK))
+        xw_all = held.tile([P, T], I32, name="xw_all")
+        nc.sync.dma_start(xw_all[:], x_words[0].rearrange("p n r -> p (n r)").bitcast(I32))
+        w2_raw = [load_weight_half(w2, 0)]
+        for q in range(4):
+            nc.vector.tensor_copy(xs_all[32 * q : 32 * q + 4, :].bitcast(I32), xs_rows[32 * q : 32 * q + 4, :].bitcast(I32))
         offs_l = load_list("offs_l", offs)
+        w2_raw.append(load_weight_half(w2, 1))
         n2_l = load_list("n2_l", n2)
         n3_l = load_list("n3_l", n3)
         n1_l = load_list("n1_l", n1)
@@ -82,10 +79,9 @@ def tile_picked_kqtwicphoporder_none_p_kernel(
             nc.vector.tensor_copy(scales[:], xs_all[:].indirect(lst[:]))
             return scales
 
-        def pick_words(name, lst):
-            words = held.tile([P, N], U32, name=name, align_bytes=64)
-            for h in range(2):
-                nc.vector.tensor_copy(words[:, HALF * h : HALF * (h + 1)], xw_all[:].bitcast(U32).indirect(half_of(lst, h)))
+        def pick_words(name, lst, tag):
+            words = held.tile([P, N], U32, name=name, tag=tag, align_bytes=64)
+            nc.vector.tensor_copy(words[:], xw_all[:].bitcast(U32).indirect(lst[:]))
             return words
 
         def deal(copy, dst, src, m0, m1, src0):
@@ -120,37 +116,39 @@ def tile_picked_kqtwicphoporder_none_p_kernel(
             )
             return bank
 
+        nc.vector.scalar_tensor_tensor(step[:], ga_t[:], 0.0, gb_t[:], ALU.is_ge, ALU.mult)
+        nc.vector.scalar_tensor_tensor(gb_full[:], step[:], 2.0, gb_t[:], ALU.mult, ALU.subtract)
+        nc.scalar.activation(gb_half[:], gb_full[:], ACT.Copy, scale=0.5)
+        nc.scalar.activation(ga_abs[:], ga_t[:], ACT.Abs)
         xt_s = pick_scales("xt_s", two_l)
+        xt_w = pick_words("xt_w", two_l, "xt_w")
+        xo_s = pick_scales("xo_s", offs_l)
         w2_g, w2_w, w2_s = mx_tiles("w2")
         deal(nc.scalar.copy, w2_g, w2_raw[0][:], 0, 64, 0)
         deal(nc.scalar.copy, w2_g, w2_raw[1][:], 64, 96, 64)
         deal(nc.vector.tensor_copy, w2_g, w2_raw[1][:], 96, 128, 64)
-        quantise(w2_g, w2_w, w2_s, 0, 4)
-        w1_raw = load_weight(w1)
-        xt_w = pick_words("xt_w", two_l)
-        nc.vector.tensor_scalar(step[:], ga_t[:], 0.0, -0.5, ALU.is_ge, ALU.add)
-        nc.vector.scalar_tensor_tensor(ga_abs[:], ga_t[:], -1.0, ga_t[:], ALU.mult, ALU.max)
-        nc.vector.tensor_tensor(gb_half[:], step[:], gb_t[:], ALU.mult)
-        nc.vector.tensor_scalar(gb_full[:], gb_half[:], 2.0, None, ALU.mult)
-        xo_s = pick_scales("xo_s", offs_l)
-        xo_w = pick_words("xo_w", offs_l)
+        for t0, t1 in ((0, 1), (1, 2), (2, 4)):
+            quantise(w2_g, w2_w, w2_s, t0, t1)
+        w1_raw = [load_weight_half(w1, 0), load_weight_half(w1, 1)]
+        xo_w = pick_words("xo_w", offs_l, "w2_g")
 
         st2 = []
         st2_copy = []
         for t in range(PACK):
-            b_half = held.tile([P, N], F32, name="b_half%d" % t)
+            b_half = held.tile([P, 2 * N], F32, name="b_half%d" % t)
             b_full = held.tile([P, N], F32, name="b_full%d" % t)
-            width = HALF if t == 0 else N
+            width = N
             for c in range(0, N, width):
                 cols = slice(c, c + width)
                 bank = product("bank", w2_w, w2_s, xt_w, xt_s, t, cols)
                 nc.scalar.activation(b_half[:, cols], bank[:], ACT.Copy, scale=gb_half[:, t : t + 1])
-                nc.scalar.activation(b_full[:, cols], bank[:], ACT.Copy, scale=gb_full[:, t : t + 1])
+                if t == 0:
+                    nc.vector.tensor_scalar(b_full[:], b_half[:, :N], 2.0, None, ALU.mult)
+                else:
+                    nc.scalar.activation(b_full[:, cols], bank[:], ACT.Copy, scale=gb_full[:, t : t + 1])
             s2 = held.tile([P, N], F32, name="st2_%d" % t)
             s2c = held.tile([P, N], F32, name="st2c_%d" % t)
-            for h in range(2):
-                cols = slice(HALF * h, HALF * (h + 1))
-                nc.vector.tensor_tensor(s2[:, cols], b_half[:].indirect(half_of(n2_l, h)), b_full[:, cols], ALU.add)
+            nc.vector.tensor_tensor(s2[:], b_half[:].indirect(n2_l[:]), b_full[:], ALU.add)
             nc.sync.dma_start(s2c[:], s2[:])
             st2.append(s2)
             st2_copy.append(s2c)
@@ -237,29 +235,32 @@ def tile_picked_kqtwicphoporder_none_p_kernel(
             quantise(z_g, z_w, z_s, t0, t1)
 
         out_rows = out.rearrange("(m t) v -> t m v", t=PACK)
-        pending = []
-
-        def put_back(t, pa, up, down):
-            res = held.tile([P, N], F32, name="res%d" % t)
-            nc.vector.tensor_tensor(res[:].indirect(n4_l[:]), pa[:], up[:], ALU.add)
-            nc.vector.tensor_tensor(res[:].indirect(n5_l[:]), pa[:], down[:], ALU.add)
-            nc.sync.dma_start(out_rows[t], res[:])
-
+        s_sb = []
         for t in range(PACK):
             bank = product("bank", z_w, z_s, z2_w, z2_s, t)
-            s_sb = held.tile([P, N], F32, name="s%d" % t)
-            nc.scalar.activation(s_sb[:], bank[:], ACT.Copy, scale=-0.0625)
-            pa = held.tile([P, HALF], F32, name="pa%d" % t)
-            gap = held.tile([P, HALF], F32, name="gap%d" % t)
-            up = held.tile([P, HALF], F32, name="up%d" % t)
-            lack = held.tile([P, HALF], F32, name="lack%d" % t)
-            down = held.tile([P, HALF], F32, name="down%d" % t)
-            nc.vector.tensor_copy(pa[:], s_sb[:].indirect(n4_l[:]))
-            nc.vector.tensor_tensor(gap[:], s_sb[:].indirect(n5_l[:]), pa[:], ALU.subtract)
-            nc.scalar.activation(up[:], gap[:], ACT.Relu)
-            nc.scalar.activation(lack[:], gap[:], ACT.Relu, scale=-1.0)
-            nc.scalar.activation(down[:], lack[:], ACT.Copy, scale=-1.0)
-            if pending:
-                put_back(*pending.pop())
-            pending.append((t, pa, up, down))
-        put_back(*pending.pop())
+            s_t = held.tile([P, N], F32, name="s%d" % t)
+            nc.scalar.activation(s_t[:], bank[:], ACT.Copy, scale=-0.0625)
+            s_sb.append(s_t)
+        pa = held.tile([P, PACK, HALF], F32, name="pa")
+        gap = held.tile([P, PACK, HALF], F32, name="gap")
+        up = held.tile([P, PACK, HALF], F32, name="up")
+        lack = held.tile([P, PACK, HALF], F32, name="lack")
+        down = held.tile([P, PACK, HALF], F32, name="down")
+        for t in range(PACK):
+            for h in range(2):
+                nc.vector.tensor_copy(pa[:, t, P * h : P * (h + 1)], s_sb[t][:].indirect(n4_l[:, 8 * h : 8 * (h + 1)]))
+            for h in range(2):
+                cols = slice(P * h, P * (h + 1))
+                nc.vector.tensor_tensor(gap[:, t, cols], s_sb[t][:].indirect(n5_l[:, 8 * h : 8 * (h + 1)]), pa[:, t, cols], ALU.subtract)
+        res = []
+        for t in range(PACK + 1):
+            if t < PACK:
+                res.append(held.tile([P, N], F32, name="res%d" % t))
+                nc.scalar.activation(up[:, t, :], gap[:, t, :], ACT.Relu)
+                nc.vector.tensor_tensor(res[t][:].indirect(n4_l[:]), pa[:, t, :], up[:, t, :], ALU.add)
+            if t > 0:
+                u = t - 1
+                nc.scalar.activation(lack[:, u, :], gap[:, u, :], ACT.Relu, scale=-1.0)
+                nc.scalar.activation(down[:, u, :], lack[:, u, :], ACT.Copy, scale=-1.0)
+                nc.vector.tensor_tensor(res[u][:].indirect(n5_l[:]), pa[:, u, :], down[:, u, :], ALU.add)
+                nc.sync.dma_start(out_rows[u], res[u][:])

@@ -16,7 +16,11 @@ P = 128
 PACK = 4
 T = 2048
 N = 512
-HALF = 256
+HALF = N // 2
+QUARTER = N // 4
+WIDE = 2 * N
+PER_COLUMN = 16
+BANKS = 8
 FLOPS = 3 * 2 * 512 * 512 * 512
 
 
@@ -26,15 +30,69 @@ def tile_picked_kqtwicphoporder_none_p_kernel(
     nc = tc.nc
     with ExitStack() as ctx:
         held = ctx.enter_context(tc.tile_pool(name="held", bufs=1))
-        psum = ctx.enter_context(tc.psum_pool(name="psum", bufs=8))
+        psum = ctx.enter_context(tc.psum_pool(name="psum", bufs=BANKS))
 
         def load_list(name, src):
             tile = held.tile(list(src.shape), U16, name=name)
             nc.sync.dma_start(tile[:], src)
             return tile
 
-        def half_of(lst, h):
-            return lst[:, 16 * h : 16 * (h + 1)]
+        def entries(lst, c0, c1):
+            return lst[:, c0 // PER_COLUMN : c1 // PER_COLUMN]
+
+        def load_weight_half(name, w, h):
+            raw = held.tile([P, PACK, HALF], F32, name="%s_raw%d" % (name, h))
+            nc.sync.dma_start(raw[:], w.rearrange("(p j) c -> p j c", j=PACK)[:, :, HALF * h : HALF * (h + 1)])
+            return raw
+
+        def load_factor(name, g):
+            tile = held.tile([P, PACK], F32, name=name)
+            nc.sync.dma_start(tile[:], g.rearrange("(p t) o -> p (t o)", t=PACK))
+            return tile
+
+        def pick_scales(name, lst):
+            scales = held.tile([P, N], U8, name=name, align_bytes=64)
+            nc.vector.tensor_copy(scales[:], xs_all[:].indirect(lst[:]))
+            return scales
+
+        def pick_words(name, lst):
+            words = held.tile([P, N], U32, name=name, align_bytes=64)
+            nc.vector.tensor_copy(words[:], xw_all[:].bitcast(U32).indirect(lst[:]))
+            return words
+
+        def stationary_tiles(name):
+            dealt = held.tile([P, PACK, P, PACK], BF16, name=name + "_dealt", align_bytes=64)
+            words = held.tile([P, N], U32, name=name + "_words", align_bytes=64)
+            scales = held.tile([P, N], U8, name=name + "_scales", align_bytes=64)
+            return dealt, words, scales
+
+        def deal_weight(copy, dealt, raw, c0, c1):
+            cols = raw[c0 // HALF][:, :, c0 % HALF : (c1 - 1) % HALF + 1]
+            copy(
+                dealt[:, :, c0 // PACK : c1 // PACK, :].rearrange("p t m j -> p m j t"),
+                cols.rearrange("p j (m t) -> p m j t", t=PACK),
+            )
+
+        def quantise(operand, t0, t1):
+            dealt, words, scales = operand
+            nc.vector.quantize_mx(
+                out=words[:, P * t0 : P * t1].bitcast(FP8X4),
+                scales=scales[:, P * t0 : P * t1],
+                in_=dealt[:, t0:t1].rearrange("p t m j -> p (t m j)"),
+            )
+
+        def product(operand, t, words, scales, c0, c1):
+            bank = psum.tile([P, c1 - c0], F32, name="bank")
+            nc.tensor.matmul_mx(
+                out=bank[:],
+                lhsT=operand[1][:, P * t : P * (t + 1)].bitcast(FP8X4),
+                lhsT_scale=operand[2][:, P * t : P * (t + 1)],
+                rhs=words[:, c0:c1].bitcast(FP8X4),
+                rhs_scale=scales[:, c0:c1],
+                start=True,
+                stop=True,
+            )
+            return bank
 
         xs_all = held.tile([P, T], U8, name="xs_all")
         nc.vector.memset(xs_all[:].bitcast(U32), 0)
@@ -43,224 +101,148 @@ def tile_picked_kqtwicphoporder_none_p_kernel(
         warm_out = held.tile([P, 1], F32, name="warm_out")
         nc.scalar.activation(warm_out[:], warm[:], ACT.Sigmoid)
 
-        def load_weight_half(w, h):
-            raw = held.tile([P, PACK, HALF], F32, name="w_raw%d" % h)
-            nc.sync.dma_start(raw[:], w.rearrange("(p j) c -> p j c", j=PACK)[:, :, HALF * h : HALF * (h + 1)])
-            return raw
-
         xs_rows = held.tile([P, T], U8, name="xs_rows")
         for q in range(4):
             nc.sync.dma_start(xs_rows[32 * q : 32 * q + 4, :].bitcast(I32), x_scales[0, 4 * q : 4 * q + 4, :].bitcast(I32))
         two_l = load_list("two_l", two)
-        gb_t = held.tile([P, PACK], F32, name="gb_t")
-        ga_t = held.tile([P, PACK], F32, name="ga_t")
-        nc.sync.dma_start(gb_t[:], gb.rearrange("(p t) o -> p (t o)", t=PACK))
-        nc.sync.dma_start(ga_t[:], ga.rearrange("(p t) o -> p (t o)", t=PACK))
+        w2_raw = [load_weight_half("w2", w2, h) for h in range(2)]
+        gb_t = load_factor("gb_t", gb)
+        ga_t = load_factor("ga_t", ga)
+        offs_l = load_list("offs_l", offs)
         xw_all = held.tile([P, T], I32, name="xw_all")
         nc.sync.dma_start(xw_all[:], x_words[0].rearrange("p n r -> p (n r)").bitcast(I32))
-        w2_raw = [load_weight_half(w2, 0)]
+        n2_l = load_list("n2_l", n2)
+        w1_raw = [load_weight_half("w1", w1, h) for h in range(2)]
         for q in range(4):
             nc.vector.tensor_copy(xs_all[32 * q : 32 * q + 4, :].bitcast(I32), xs_rows[32 * q : 32 * q + 4, :].bitcast(I32))
-        offs_l = load_list("offs_l", offs)
-        w2_raw.append(load_weight_half(w2, 1))
-        n2_l = load_list("n2_l", n2)
         n3_l = load_list("n3_l", n3)
         n1_l = load_list("n1_l", n1)
         n4_l = load_list("n4_l", n4)
         n5_l = load_list("n5_l", n5)
 
-        step = held.tile([P, PACK], F32, name="step")
-        ga_abs = held.tile([P, PACK], F32, name="ga_abs")
+        two_scales = pick_scales("two_scales", two_l)
+
+        gb_where = held.tile([P, PACK], F32, name="gb_where")
         gb_full = held.tile([P, PACK], F32, name="gb_full")
         gb_half = held.tile([P, PACK], F32, name="gb_half")
-
-        def pick_scales(name, lst):
-            scales = held.tile([P, N], U8, name=name, align_bytes=64)
-            nc.vector.tensor_copy(scales[:], xs_all[:].indirect(lst[:]))
-            return scales
-
-        def pick_words(name, lst, tag):
-            words = held.tile([P, N], U32, name=name, tag=tag, align_bytes=64)
-            nc.vector.tensor_copy(words[:], xw_all[:].bitcast(U32).indirect(lst[:]))
-            return words
-
-        def deal(copy, dst, src, m0, m1, src0):
-            copy(
-                dst[:, :, m0:m1, :].rearrange("p t m j -> p m j t"),
-                src.rearrange("p j (m t) -> p m j t", t=PACK)[:, m0 - src0 : m1 - src0, :, :],
-            )
-
-        def mx_tiles(name):
-            grouped = held.tile([P, PACK, P, PACK], BF16, name=name + "_g", align_bytes=64)
-            words = held.tile([P, N], U32, name=name + "_w", align_bytes=64)
-            scales = held.tile([P, N], U8, name=name + "_s", align_bytes=64)
-            return grouped, words, scales
-
-        def quantise(grouped, words, scales, t0, t1):
-            nc.vector.quantize_mx(
-                out=words[:, P * t0 : P * t1].bitcast(FP8X4),
-                scales=scales[:, P * t0 : P * t1],
-                in_=grouped[:, t0:t1].rearrange("p t m j -> p (t m j)"),
-            )
-
-        def product(tag, lw, ls, rw, rs, t, cols=slice(0, N)):
-            bank = psum.tile([P, cols.stop - cols.start], F32, name=tag)
-            nc.tensor.matmul_mx(
-                out=bank[:],
-                lhsT=lw[:, P * t : P * (t + 1)].bitcast(FP8X4),
-                lhsT_scale=ls[:, P * t : P * (t + 1)],
-                rhs=rw[:, cols].bitcast(FP8X4),
-                rhs_scale=rs[:, cols],
-                start=True,
-                stop=True,
-            )
-            return bank
-
-        nc.vector.scalar_tensor_tensor(step[:], ga_t[:], 0.0, gb_t[:], ALU.is_ge, ALU.mult)
-        nc.vector.scalar_tensor_tensor(gb_full[:], step[:], 2.0, gb_t[:], ALU.mult, ALU.subtract)
+        ga_abs = held.tile([P, PACK], F32, name="ga_abs")
+        nc.vector.scalar_tensor_tensor(gb_where[:], ga_t[:], 0.0, gb_t[:], ALU.is_ge, ALU.mult)
+        nc.vector.scalar_tensor_tensor(gb_full[:], gb_where[:], 2.0, gb_t[:], ALU.mult, ALU.subtract)
         nc.scalar.activation(gb_half[:], gb_full[:], ACT.Copy, scale=0.5)
         nc.scalar.activation(ga_abs[:], ga_t[:], ACT.Abs)
-        xt_s = pick_scales("xt_s", two_l)
-        xt_w = pick_words("xt_w", two_l, "xt_w")
-        xo_s = pick_scales("xo_s", offs_l)
-        w2_g, w2_w, w2_s = mx_tiles("w2")
-        deal(nc.scalar.copy, w2_g, w2_raw[0][:], 0, 64, 0)
-        deal(nc.scalar.copy, w2_g, w2_raw[1][:], 64, 96, 64)
-        deal(nc.vector.tensor_copy, w2_g, w2_raw[1][:], 96, 128, 64)
-        for t0, t1 in ((0, 1), (1, 2), (2, 4)):
-            quantise(w2_g, w2_w, w2_s, t0, t1)
-        w1_raw = [load_weight_half(w1, 0), load_weight_half(w1, 1)]
-        xo_w = pick_words("xo_w", offs_l, "w2_g")
 
+        offs_scales = pick_scales("offs_scales", offs_l)
+        w2_mx = stationary_tiles("w2")
+        for c0 in (0, HALF):
+            deal_weight(nc.scalar.copy, w2_mx[0], w2_raw, c0, c0 + HALF)
+        quantise(w2_mx, 0, PACK)
+        two_words = pick_words("two_words", two_l)
+        offs_words = pick_words("offs_words", offs_l)
+
+        w1_mx = stationary_tiles("w1")
         st2 = []
-        st2_copy = []
+        st2_again = []
         for t in range(PACK):
-            b_half = held.tile([P, 2 * N], F32, name="b_half%d" % t)
+            b_half = held.tile([P, WIDE], F32, name="b_half%d" % t)
             b_full = held.tile([P, N], F32, name="b_full%d" % t)
-            width = N
-            for c in range(0, N, width):
-                cols = slice(c, c + width)
-                bank = product("bank", w2_w, w2_s, xt_w, xt_s, t, cols)
-                nc.scalar.activation(b_half[:, cols], bank[:], ACT.Copy, scale=gb_half[:, t : t + 1])
-                if t == 0:
-                    nc.vector.tensor_scalar(b_full[:], b_half[:, :N], 2.0, None, ALU.mult)
-                else:
-                    nc.scalar.activation(b_full[:, cols], bank[:], ACT.Copy, scale=gb_full[:, t : t + 1])
-            s2 = held.tile([P, N], F32, name="st2_%d" % t)
-            s2c = held.tile([P, N], F32, name="st2c_%d" % t)
-            nc.vector.tensor_tensor(s2[:], b_half[:].indirect(n2_l[:]), b_full[:], ALU.add)
-            nc.sync.dma_start(s2c[:], s2[:])
-            st2.append(s2)
-            st2_copy.append(s2c)
+            bank = product(w2_mx, t, two_words, two_scales, 0, N)
+            nc.scalar.activation(b_half[:, :N], bank[:], ACT.Copy, scale=gb_half[:, t : t + 1])
+            if t == 0:
+                nc.vector.tensor_scalar(b_full[:], b_half[:, :N], 2.0, None, ALU.mult)
+            else:
+                nc.scalar.activation(b_full[:], bank[:], ACT.Copy, scale=gb_full[:, t : t + 1])
+            st2.append(held.tile([P, N], F32, name="st2_%d" % t))
+            st2_again.append(held.tile([P, N], F32, name="st2_again%d" % t))
+            nc.vector.tensor_tensor(st2[t][:], b_half[:].indirect(n2_l[:]), b_full[:], ALU.add)
+            nc.sync.dma_start(st2_again[t][:], st2[t][:])
+            if t == 1:
+                for c0 in (0, QUARTER):
+                    deal_weight(nc.scalar.copy, w1_mx[0], w1_raw, c0, c0 + QUARTER)
+                for c0 in (HALF, HALF + QUARTER):
+                    deal_weight(nc.vector.tensor_copy, w1_mx[0], w1_raw, c0, c0 + QUARTER)
+                for t0, t1 in ((0, 1), (1, 2), (2, PACK)):
+                    quantise(w1_mx, t0, t1)
 
-        w1_g, w1_w, w1_s = mx_tiles("w1")
-        deal(nc.scalar.copy, w1_g, w1_raw[0][:], 0, 64, 0)
-        deal(nc.scalar.copy, w1_g, w1_raw[1][:], 64, 128, 64)
-
-        z2 = []
-        for h in range(2):
-            cols = slice(HALF * h, HALF * (h + 1))
-            if h == 1:
-                quantise(w1_g, w1_w, w1_s, 0, 1)
-                quantise(w1_g, w1_w, w1_s, 1, 2)
-                quantise(w1_g, w1_w, w1_s, 2, 4)
-            z2_h = held.tile([P, PACK, HALF], F32, name="z2_%d" % h, tag=("z2_0", "w1_g")[h], align_bytes=64)
-            for t in range(PACK):
-                nc.vector.tensor_tensor(z2_h[:, t, :], st2[t][:].indirect(half_of(n3_l, h)), st2_copy[t][:, cols], ALU.subtract)
-            z2.append(z2_h)
-
-        z2_w = held.tile([P, N], U32, name="z2_w", align_bytes=64)
-        z2_s = held.tile([P, N], U8, name="z2_s", align_bytes=64)
-
-        def weave_z2(h, tag):
-            grouped = held.tile([P, HALF, PACK], BF16, name="z2_g%d" % h, tag=tag, align_bytes=64)
-            nc.scalar.copy(
-                grouped[:].rearrange("p (c i) t -> p c t i", i=4),
-                z2[h][:].rearrange("p t (c i) -> p c t i", i=4),
-            )
-            return grouped
-
-        def quantise_z2(h, grouped):
-            cols = slice(HALF * h, HALF * (h + 1))
-            nc.vector.quantize_mx(out=z2_w[:, cols].bitcast(FP8X4), scales=z2_s[:, cols], in_=grouped[:].rearrange("p c t -> p (c t)"))
-
-        z2_g0 = weave_z2(0, "z2_g0")
-
+        gate = held.tile([P, PACK, N], F32, name="gate")
+        st_looked = held.tile([P, PACK, N], BF16, name="st_looked")
+        st_plain = held.tile([P, PACK, N], BF16, name="st_plain")
         z = held.tile([P, PACK, N], BF16, name="z")
         st = []
-        looked = held.tile([P, PACK, N], F32, name="looked")
-
-        def larger(t, h):
-            cols = slice(HALF * h, HALF * (h + 1))
-            nc.vector.tensor_copy(looked[:, t, cols], st[t][:].indirect(half_of(n1_l, h)))
-
-        def larger2(t, h):
-            cols = slice(HALF * h, HALF * (h + 1))
-            nc.vector.tensor_tensor(z[:, t, cols], st[t][:, cols], looked[:, t, cols], ALU.max)
-
         for t in range(PACK):
-            bank = product("bank", w1_w, w1_s, xo_w, xo_s, t)
-            a_sb = held.tile([P, N], F32, name="a%d" % t, align_bytes=64)
-            nc.scalar.copy(a_sb[:], bank[:])
-            gate = held.tile([P, N], F32, name="gate%d" % t)
-            for h in range(2):
-                cols = slice(HALF * h, HALF * (h + 1))
-                nc.scalar.activation(gate[:, cols], a_sb[:].indirect(half_of(n1_l, h)), ACT.Sigmoid)
-            s1 = held.tile([P, N], F32, name="st%d" % t)
-            nc.vector.scalar_tensor_tensor(s1[:], bank[:], ga_abs[:, t : t + 1], gate[:], ALU.mult, ALU.mult)
-            st.append(s1)
-            if t in (1, 2):
-                larger2(t - 1, 1)
-            larger(t, 0)
-            if t == 3:
-                larger2(2, 0)
-            if t < 2:
-                larger(t, 1)
-                larger2(t, 0)
-            if t == 0:
-                quantise_z2(0, z2_g0)
-
-        z2_g1 = weave_z2(1, "a3")
-        z_g, z_w, z_s = mx_tiles("z")
-        larger(2, 1)
-        larger2(3, 0)
-        deal(nc.scalar.copy, z_g, z[:], 0, 64, 0)
-        larger(3, 1)
-        larger2(2, 1)
-        quantise_z2(1, z2_g1)
-        larger2(3, 1)
-        deal(nc.scalar.copy, z_g, z[:], 64, 88, 0)
-        deal(nc.vector.tensor_copy, z_g, z[:], 88, 128, 0)
-        for t0, t1 in ((0, 1), (1, 2), (2, 4)):
-            quantise(z_g, z_w, z_s, t0, t1)
-
-        out_rows = out.rearrange("(m t) v -> t m v", t=PACK)
-        s_sb = []
+            bank = product(w1_mx, t, offs_words, offs_scales, 0, N)
+            a = held.tile([P, WIDE], F32, name="a%d" % t)
+            nc.scalar.copy(a[:, :N], bank[:])
+            nc.scalar.activation(gate[:, t, :], a[:].indirect(n1_l[:]), ACT.Sigmoid)
+            st.append(held.tile([P, WIDE], F32, name="st%d" % t))
+            nc.vector.scalar_tensor_tensor(st[t][:, :N], bank[:], ga_abs[:, t : t + 1], gate[:, t, :], ALU.mult, ALU.mult)
+            nc.vector.tensor_copy(st_looked[:, t, :], st[t][:].indirect(n1_l[:]))
         for t in range(PACK):
-            bank = product("bank", z_w, z_s, z2_w, z2_s, t)
-            s_t = held.tile([P, N], F32, name="s%d" % t)
-            nc.scalar.activation(s_t[:], bank[:], ACT.Copy, scale=-0.0625)
-            s_sb.append(s_t)
+            nc.scalar.copy(st_plain[:, t, :], st[t][:, :N])
+            nc.vector.tensor_tensor(z[:, t, :], st_plain[:, t, :], st_looked[:, t, :], ALU.max)
+
+        z_mx = stationary_tiles("z")
+        z2_words = held.tile([P, N], U32, name="z2_words", align_bytes=64)
+        z2_scales = held.tile([P, N], U8, name="z2_scales", align_bytes=64)
+
+        def deal_z(t):
+            nc.scalar.copy(z_mx[0][:, t], z[:].rearrange("p j (m t) -> p t m j", t=PACK)[:, t])
+
+        def make_z2(c0, c1, tag, copy):
+            minus_z2 = held.tile([P, PACK, c1 - c0], F32, name="minus_z2_%d" % c0, tag=tag)
+            for t in range(PACK):
+                nc.vector.tensor_tensor(
+                    minus_z2[:, t, :], st2[t][:].indirect(entries(n3_l, c0, c1)), st2_again[t][:, c0:c1], ALU.subtract
+                )
+            woven = held.tile([P, c1 - c0, PACK], BF16, name="woven%d" % c0, align_bytes=64)
+            copy(woven[:].rearrange("p (c i) t -> p c t i", i=4), minus_z2[:].rearrange("p t (c i) -> p c t i", i=4))
+            nc.vector.quantize_mx(
+                out=z2_words[:, c0:c1].bitcast(FP8X4),
+                scales=z2_scales[:, c0:c1],
+                in_=woven[:].rearrange("p c t -> p (c t)"),
+            )
+
+        s = [held.tile([P, N], F32, name="s%d" % t) for t in range(PACK)]
+
+        def make_s(t, c0, c1):
+            bank = product(z_mx, t, z2_words, z2_scales, c0, c1)
+            nc.scalar.activation(s[t][:, c0:c1], bank[:], ACT.Copy, scale=-0.0625)
+
+        make_z2(0, HALF, "minus_z2_first", nc.scalar.copy)
+        deal_z(0)
+        quantise(z_mx, 0, 1)
+        make_z2(HALF, HALF + QUARTER, "st_looked", nc.scalar.copy)
+        for t in range(1, PACK):
+            deal_z(t)
+        make_z2(HALF + QUARTER, N, "st_plain", nc.vector.tensor_copy)
+        for c0, c1 in ((0, HALF), (HALF, HALF + QUARTER), (HALF + QUARTER, N)):
+            make_s(0, c0, c1)
+        for t in range(1, PACK):
+            quantise(z_mx, t, t + 1)
+            make_s(t, 0, N)
+
         pa = held.tile([P, PACK, HALF], F32, name="pa")
         gap = held.tile([P, PACK, HALF], F32, name="gap")
         up = held.tile([P, PACK, HALF], F32, name="up")
         lack = held.tile([P, PACK, HALF], F32, name="lack")
         down = held.tile([P, PACK, HALF], F32, name="down")
         for t in range(PACK):
-            for h in range(2):
-                nc.vector.tensor_copy(pa[:, t, P * h : P * (h + 1)], s_sb[t][:].indirect(n4_l[:, 8 * h : 8 * (h + 1)]))
-            for h in range(2):
-                cols = slice(P * h, P * (h + 1))
-                nc.vector.tensor_tensor(gap[:, t, cols], s_sb[t][:].indirect(n5_l[:, 8 * h : 8 * (h + 1)]), pa[:, t, cols], ALU.subtract)
-        res = []
+            for c0 in (0, QUARTER):
+                nc.vector.tensor_copy(pa[:, t, c0 : c0 + QUARTER], s[t][:].indirect(entries(n4_l, c0, c0 + QUARTER)))
+            for c0 in (0, QUARTER):
+                cols = slice(c0, c0 + QUARTER)
+                nc.vector.tensor_tensor(
+                    gap[:, t, cols], s[t][:].indirect(entries(n5_l, c0, c0 + QUARTER)), pa[:, t, cols], ALU.subtract
+                )
+        out_rows = out.rearrange("(m t) v -> t m v", t=PACK)
+        placed = []
         for t in range(PACK + 1):
             if t < PACK:
-                res.append(held.tile([P, N], F32, name="res%d" % t))
+                placed.append(held.tile([P, N], F32, name="placed%d" % t))
                 nc.scalar.activation(up[:, t, :], gap[:, t, :], ACT.Relu)
-                nc.vector.tensor_tensor(res[t][:].indirect(n4_l[:]), pa[:, t, :], up[:, t, :], ALU.add)
+                nc.vector.tensor_tensor(placed[t][:].indirect(n4_l[:]), pa[:, t, :], up[:, t, :], ALU.add)
             if t > 0:
                 u = t - 1
                 nc.scalar.activation(lack[:, u, :], gap[:, u, :], ACT.Relu, scale=-1.0)
                 nc.scalar.activation(down[:, u, :], lack[:, u, :], ACT.Copy, scale=-1.0)
-                nc.vector.tensor_tensor(res[u][:].indirect(n5_l[:]), pa[:, u, :], down[:, u, :], ALU.add)
-                nc.sync.dma_start(out_rows[u], res[u][:])
+                nc.vector.tensor_tensor(placed[u][:].indirect(n5_l[:]), pa[:, u, :], down[:, u, :], ALU.add)
+                nc.sync.dma_start(out_rows[u], placed[u][:])

@@ -55,8 +55,8 @@ def tile_picked_kqtwicphoporder_none_p_kernel(
             nc.vector.tensor_copy(scales[:], xs_all[:].indirect(lst[:]))
             return scales
 
-        def pick_words(name, lst):
-            words = held.tile([P, N], U32, name=name, align_bytes=64)
+        def pick_words(name, lst, tag):
+            words = held.tile([P, N], U32, name=name, tag=tag, align_bytes=64)
             nc.vector.tensor_copy(words[:], xw_all[:].bitcast(U32).indirect(lst[:]))
             return words
 
@@ -105,16 +105,17 @@ def tile_picked_kqtwicphoporder_none_p_kernel(
         for q in range(4):
             nc.sync.dma_start(xs_rows[32 * q : 32 * q + 4, :].bitcast(I32), x_scales[0, 4 * q : 4 * q + 4, :].bitcast(I32))
         two_l = load_list("two_l", two)
-        w2_raw = [load_weight_half("w2", w2, h) for h in range(2)]
         gb_t = load_factor("gb_t", gb)
         ga_t = load_factor("ga_t", ga)
-        offs_l = load_list("offs_l", offs)
         xw_all = held.tile([P, T], I32, name="xw_all")
         nc.sync.dma_start(xw_all[:], x_words[0].rearrange("p n r -> p (n r)").bitcast(I32))
-        n2_l = load_list("n2_l", n2)
-        w1_raw = [load_weight_half("w1", w1, h) for h in range(2)]
+        w2_raw = [load_weight_half("w2", w2, 0)]
         for q in range(4):
             nc.vector.tensor_copy(xs_all[32 * q : 32 * q + 4, :].bitcast(I32), xs_rows[32 * q : 32 * q + 4, :].bitcast(I32))
+        offs_l = load_list("offs_l", offs)
+        w2_raw.append(load_weight_half("w2", w2, 1))
+        n2_l = load_list("n2_l", n2)
+        w1_raw = [load_weight_half("w1", w1, h) for h in range(2)]
         n3_l = load_list("n3_l", n3)
         n1_l = load_list("n1_l", n1)
         n4_l = load_list("n4_l", n4)
@@ -127,17 +128,19 @@ def tile_picked_kqtwicphoporder_none_p_kernel(
         gb_half = held.tile([P, PACK], F32, name="gb_half")
         ga_abs = held.tile([P, PACK], F32, name="ga_abs")
         nc.vector.scalar_tensor_tensor(gb_where[:], ga_t[:], 0.0, gb_t[:], ALU.is_ge, ALU.mult)
+        two_words = pick_words("two_words", two_l, "two_words")
         nc.vector.scalar_tensor_tensor(gb_full[:], gb_where[:], 2.0, gb_t[:], ALU.mult, ALU.subtract)
         nc.scalar.activation(gb_half[:], gb_full[:], ACT.Copy, scale=0.5)
         nc.scalar.activation(ga_abs[:], ga_t[:], ACT.Abs)
 
         offs_scales = pick_scales("offs_scales", offs_l)
         w2_mx = stationary_tiles("w2")
-        for c0 in (0, HALF):
-            deal_weight(nc.scalar.copy, w2_mx[0], w2_raw, c0, c0 + HALF)
-        quantise(w2_mx, 0, PACK)
-        two_words = pick_words("two_words", two_l)
-        offs_words = pick_words("offs_words", offs_l)
+        deal_weight(nc.scalar.copy, w2_mx[0], w2_raw, 0, HALF)
+        deal_weight(nc.scalar.copy, w2_mx[0], w2_raw, HALF, HALF + QUARTER)
+        deal_weight(nc.vector.tensor_copy, w2_mx[0], w2_raw, HALF + QUARTER, N)
+        for t0, t1 in ((0, 1), (1, 2), (2, PACK)):
+            quantise(w2_mx, t0, t1)
+        offs_words = pick_words("offs_words", offs_l, "w2_dealt")
 
         w1_mx = stationary_tiles("w1")
         st2 = []
@@ -156,10 +159,9 @@ def tile_picked_kqtwicphoporder_none_p_kernel(
             nc.vector.tensor_tensor(st2[t][:], b_half[:].indirect(n2_l[:]), b_full[:], ALU.add)
             nc.sync.dma_start(st2_again[t][:], st2[t][:])
             if t == 1:
-                for c0 in (0, QUARTER):
+                for c0 in (0, QUARTER, HALF):
                     deal_weight(nc.scalar.copy, w1_mx[0], w1_raw, c0, c0 + QUARTER)
-                for c0 in (HALF, HALF + QUARTER):
-                    deal_weight(nc.vector.tensor_copy, w1_mx[0], w1_raw, c0, c0 + QUARTER)
+                deal_weight(nc.vector.tensor_copy, w1_mx[0], w1_raw, HALF + QUARTER, N)
                 for t0, t1 in ((0, 1), (1, 2), (2, PACK)):
                     quantise(w1_mx, t0, t1)
 

from contextlib import ExitStack

import concourse.mybir as mybir

F32 = mybir.dt.float32
BF16 = mybir.dt.bfloat16
I32 = mybir.dt.int32
U32 = mybir.dt.uint32
U16 = mybir.dt.uint16
U8 = mybir.dt.uint8
FP8X4 = mybir.dt.float8_e4m3fn_x4
ALU = mybir.AluOpType
ACT = mybir.ActivationFunctionType

P = 128
PACK = 4
T = 2048
N = 512
HALF = N // 2
QUARTER = N // 4
WIDE = 2 * N
PER_COLUMN = 16
BANKS = 8
FLOPS = 3 * 2 * 512 * 512 * 512


def tile_picked_kqtwicphoporder_none_p_kernel(
    tc, x_words, x_scales, w1, w2, ga, gb, offs, two, n1, n2, n3, n4, n5, out
):
    nc = tc.nc
    with ExitStack() as ctx:
        held = ctx.enter_context(tc.tile_pool(name="held", bufs=1))
        psum = ctx.enter_context(tc.psum_pool(name="psum", bufs=BANKS))

        def load_list(name, src):
            tile = held.tile(list(src.shape), U16, name=name)
            nc.sync.dma_start(tile[:], src)
            return tile

        def entries(lst, c0, c1):
            return lst[:, c0 // PER_COLUMN : c1 // PER_COLUMN]

        def load_weight_half(name, w, h):
            raw = held.tile([P, PACK, HALF], F32, name="%s_raw%d" % (name, h))
            nc.sync.dma_start(raw[:], w.rearrange("(p j) c -> p j c", j=PACK)[:, :, HALF * h : HALF * (h + 1)])
            return raw

        def load_factor(name, g):
            tile = held.tile([P, PACK], F32, name=name)
            nc.sync.dma_start(tile[:], g.rearrange("(p t) o -> p (t o)", t=PACK))
            return tile

        def pick_scales(name, lst):
            scales = held.tile([P, N], U8, name=name, align_bytes=64)
            nc.vector.tensor_copy(scales[:], xs_all[:].indirect(lst[:]))
            return scales

        def pick_words(name, lst, tag):
            words = held.tile([P, N], U32, name=name, tag=tag, align_bytes=64)
            nc.vector.tensor_copy(words[:], xw_all[:].bitcast(U32).indirect(lst[:]))
            return words

        def stationary_tiles(name):
            dealt = held.tile([P, PACK, P, PACK], BF16, name=name + "_dealt", align_bytes=64)
            words = held.tile([P, N], U32, name=name + "_words", align_bytes=64)
            scales = held.tile([P, N], U8, name=name + "_scales", align_bytes=64)
            return dealt, words, scales

        def deal_weight(copy, dealt, raw, c0, c1):
            cols = raw[c0 // HALF][:, :, c0 % HALF : (c1 - 1) % HALF + 1]
            copy(
                dealt[:, :, c0 // PACK : c1 // PACK, :].rearrange("p t m j -> p m j t"),
                cols.rearrange("p j (m t) -> p m j t", t=PACK),
            )

        def quantise(operand, t0, t1):
            dealt, words, scales = operand
            nc.vector.quantize_mx(
                out=words[:, P * t0 : P * t1].bitcast(FP8X4),
                scales=scales[:, P * t0 : P * t1],
                in_=dealt[:, t0:t1].rearrange("p t m j -> p (t m j)"),
            )

        def product(operand, t, words, scales, c0, c1):
            bank = psum.tile([P, c1 - c0], F32, name="bank")
            nc.tensor.matmul_mx(
                out=bank[:],
                lhsT=operand[1][:, P * t : P * (t + 1)].bitcast(FP8X4),
                lhsT_scale=operand[2][:, P * t : P * (t + 1)],
                rhs=words[:, c0:c1].bitcast(FP8X4),
                rhs_scale=scales[:, c0:c1],
                start=True,
                stop=True,
            )
            return bank

        xs_all = held.tile([P, T], U8, name="xs_all")
        nc.vector.memset(xs_all[:].bitcast(U32), 0)
        warm = held.tile([P, 1], F32, name="warm")
        nc.gpsimd.memset(warm[:], 0.0)
        warm_out = held.tile([P, 1], F32, name="warm_out")
        nc.scalar.activation(warm_out[:], warm[:], ACT.Sigmoid)

        xs_rows = held.tile([P, T], U8, name="xs_rows")
        for q in range(4):
            nc.sync.dma_start(xs_rows[32 * q : 32 * q + 4, :].bitcast(I32), x_scales[0, 4 * q : 4 * q + 4, :].bitcast(I32))
        two_l = load_list("two_l", two)
        gb_t = load_factor("gb_t", gb)
        ga_t = load_factor("ga_t", ga)
        xw_all = held.tile([P, T], I32, name="xw_all")
        nc.sync.dma_start(xw_all[:], x_words[0].rearrange("p n r -> p (n r)").bitcast(I32))
        w2_raw = [load_weight_half("w2", w2, 0)]
        for q in range(4):
            nc.vector.tensor_copy(xs_all[32 * q : 32 * q + 4, :].bitcast(I32), xs_rows[32 * q : 32 * q + 4, :].bitcast(I32))
        offs_l = load_list("offs_l", offs)
        w2_raw.append(load_weight_half("w2", w2, 1))
        n2_l = load_list("n2_l", n2)
        w1_raw = [load_weight_half("w1", w1, h) for h in range(2)]
        n3_l = load_list("n3_l", n3)
        n1_l = load_list("n1_l", n1)
        n4_l = load_list("n4_l", n4)
        n5_l = load_list("n5_l", n5)

        two_scales = pick_scales("two_scales", two_l)

        gb_where = held.tile([P, PACK], F32, name="gb_where")
        gb_full = held.tile([P, PACK], F32, name="gb_full")
        gb_half = held.tile([P, PACK], F32, name="gb_half")
        ga_abs = held.tile([P, PACK], F32, name="ga_abs")
        nc.vector.scalar_tensor_tensor(gb_where[:], ga_t[:], 0.0, gb_t[:], ALU.is_ge, ALU.mult)
        two_words = pick_words("two_words", two_l, "two_words")
        nc.vector.scalar_tensor_tensor(gb_full[:], gb_where[:], 2.0, gb_t[:], ALU.mult, ALU.subtract)
        nc.scalar.activation(gb_half[:], gb_full[:], ACT.Copy, scale=0.5)
        nc.scalar.activation(ga_abs[:], ga_t[:], ACT.Abs)

        offs_scales = pick_scales("offs_scales", offs_l)
        w2_mx = stationary_tiles("w2")
        deal_weight(nc.scalar.copy, w2_mx[0], w2_raw, 0, HALF)
        deal_weight(nc.scalar.copy, w2_mx[0], w2_raw, HALF, HALF + QUARTER)
        deal_weight(nc.vector.tensor_copy, w2_mx[0], w2_raw, HALF + QUARTER, N)
        for t0, t1 in ((0, 1), (1, 2), (2, PACK)):
            quantise(w2_mx, t0, t1)
        offs_words = pick_words("offs_words", offs_l, "w2_dealt")

        w1_mx = stationary_tiles("w1")
        st2 = []
        st2_again = []
        for t in range(PACK):
            b_half = held.tile([P, WIDE], F32, name="b_half%d" % t)
            b_full = held.tile([P, N], F32, name="b_full%d" % t)
            bank = product(w2_mx, t, two_words, two_scales, 0, N)
            nc.scalar.activation(b_half[:, :N], bank[:], ACT.Copy, scale=gb_half[:, t : t + 1])
            if t == 0:
                nc.vector.tensor_scalar(b_full[:], b_half[:, :N], 2.0, None, ALU.mult)
            else:
                nc.scalar.activation(b_full[:], bank[:], ACT.Copy, scale=gb_full[:, t : t + 1])
            st2.append(held.tile([P, N], F32, name="st2_%d" % t))
            st2_again.append(held.tile([P, N], F32, name="st2_again%d" % t))
            nc.vector.tensor_tensor(st2[t][:], b_half[:].indirect(n2_l[:]), b_full[:], ALU.add)
            nc.sync.dma_start(st2_again[t][:], st2[t][:])
            if t == 1:
                for c0 in (0, QUARTER, HALF):
                    deal_weight(nc.scalar.copy, w1_mx[0], w1_raw, c0, c0 + QUARTER)
                deal_weight(nc.vector.tensor_copy, w1_mx[0], w1_raw, HALF + QUARTER, N)
                for t0, t1 in ((0, 1), (1, 2), (2, PACK)):
                    quantise(w1_mx, t0, t1)

        gate = held.tile([P, PACK, N], F32, name="gate")
        st_looked = held.tile([P, PACK, N], BF16, name="st_looked")
        st_plain = held.tile([P, PACK, N], BF16, name="st_plain")
        z = held.tile([P, PACK, N], BF16, name="z")
        st = []
        for t in range(PACK):
            bank = product(w1_mx, t, offs_words, offs_scales, 0, N)
            a = held.tile([P, WIDE], F32, name="a%d" % t)
            nc.scalar.copy(a[:, :N], bank[:])
            nc.scalar.activation(gate[:, t, :], a[:].indirect(n1_l[:]), ACT.Sigmoid)
            st.append(held.tile([P, WIDE], F32, name="st%d" % t))
            nc.vector.scalar_tensor_tensor(st[t][:, :N], bank[:], ga_abs[:, t : t + 1], gate[:, t, :], ALU.mult, ALU.mult)
            nc.vector.tensor_copy(st_looked[:, t, :], st[t][:].indirect(n1_l[:]))
        for t in range(PACK):
            nc.scalar.copy(st_plain[:, t, :], st[t][:, :N])
            nc.vector.tensor_tensor(z[:, t, :], st_plain[:, t, :], st_looked[:, t, :], ALU.max)

        z_mx = stationary_tiles("z")
        z2_words = held.tile([P, N], U32, name="z2_words", align_bytes=64)
        z2_scales = held.tile([P, N], U8, name="z2_scales", align_bytes=64)

        def deal_z(t):
            nc.scalar.copy(z_mx[0][:, t], z[:].rearrange("p j (m t) -> p t m j", t=PACK)[:, t])

        def make_z2(c0, c1, tag, copy):
            minus_z2 = held.tile([P, PACK, c1 - c0], F32, name="minus_z2_%d" % c0, tag=tag)
            for t in range(PACK):
                nc.vector.tensor_tensor(
                    minus_z2[:, t, :], st2[t][:].indirect(entries(n3_l, c0, c1)), st2_again[t][:, c0:c1], ALU.subtract
                )
            woven = held.tile([P, c1 - c0, PACK], BF16, name="woven%d" % c0, align_bytes=64)
            copy(woven[:].rearrange("p (c i) t -> p c t i", i=4), minus_z2[:].rearrange("p t (c i) -> p c t i", i=4))
            nc.vector.quantize_mx(
                out=z2_words[:, c0:c1].bitcast(FP8X4),
                scales=z2_scales[:, c0:c1],
                in_=woven[:].rearrange("p c t -> p (c t)"),
            )

        s = [held.tile([P, N], F32, name="s%d" % t) for t in range(PACK)]

        def make_s(t, c0, c1):
            bank = product(z_mx, t, z2_words, z2_scales, c0, c1)
            nc.scalar.activation(s[t][:, c0:c1], bank[:], ACT.Copy, scale=-0.0625)

        make_z2(0, HALF, "minus_z2_first", nc.scalar.copy)
        deal_z(0)
        quantise(z_mx, 0, 1)
        make_z2(HALF, HALF + QUARTER, "st_looked", nc.scalar.copy)
        for t in range(1, PACK):
            deal_z(t)
        make_z2(HALF + QUARTER, N, "st_plain", nc.vector.tensor_copy)
        for c0, c1 in ((0, HALF), (HALF, HALF + QUARTER), (HALF + QUARTER, N)):
            make_s(0, c0, c1)
        for t in range(1, PACK):
            quantise(z_mx, t, t + 1)
            make_s(t, 0, N)

        pa = held.tile([P, PACK, HALF], F32, name="pa")
        gap = held.tile([P, PACK, HALF], F32, name="gap")
        up = held.tile([P, PACK, HALF], F32, name="up")
        lack = held.tile([P, PACK, HALF], F32, name="lack")
        down = held.tile([P, PACK, HALF], F32, name="down")
        for t in range(PACK):
            for c0 in (0, QUARTER):
                nc.vector.tensor_copy(pa[:, t, c0 : c0 + QUARTER], s[t][:].indirect(entries(n4_l, c0, c0 + QUARTER)))
            for c0 in (0, QUARTER):
                cols = slice(c0, c0 + QUARTER)
                nc.vector.tensor_tensor(
                    gap[:, t, cols], s[t][:].indirect(entries(n5_l, c0, c0 + QUARTER)), pa[:, t, cols], ALU.subtract
                )
        out_rows = out.rearrange("(m t) v -> t m v", t=PACK)
        placed = []
        for t in range(PACK + 1):
            if t < PACK:
                placed.append(held.tile([P, N], F32, name="placed%d" % t))
                nc.scalar.activation(up[:, t, :], gap[:, t, :], ACT.Relu)
                nc.vector.tensor_tensor(placed[t][:].indirect(n4_l[:]), pa[:, t, :], up[:, t, :], ALU.add)
            if t > 0:
                u = t - 1
                nc.scalar.activation(lack[:, u, :], gap[:, u, :], ACT.Relu, scale=-1.0)
                nc.scalar.activation(down[:, u, :], lack[:, u, :], ACT.Copy, scale=-1.0)
                nc.vector.tensor_tensor(placed[u][:].indirect(n5_l[:]), pa[:, u, :], down[:, u, :], ALU.add)
                nc.sync.dma_start(out_rows[u], placed[u][:])
